import numpy as np
import ml_dtypes


def mxq(x, axis, fmt="e4m3"):
    dtype, down = {"e4m3": (ml_dtypes.float8_e4m3fn, 7), "e5m2": (ml_dtypes.float8_e5m2, 14)}[fmt]
    v = np.moveaxis(np.asarray(x, np.float32).astype(ml_dtypes.bfloat16).astype(np.float64), axis, -1)
    blocks = v.reshape(v.shape[:-1] + (-1, 32))
    amax = np.abs(blocks).max(-1, keepdims=True)
    byte = np.maximum(np.where(amax > 0, np.frexp(amax)[1] - 1 + 127, 0) - down, 1)
    scale = np.exp2(byte - 127.0)
    codes = (blocks / scale).astype(np.float32).astype(dtype).astype(np.float64)
    return np.moveaxis((codes * scale).reshape(v.shape), -1, axis)


WIDE = False


def mx_kscale(k):
    if not WIDE:
        return np.ones(k)
    levels = np.array([10, -10, 5, -5, 0])
    if k % 512:
        return np.exp2(np.random.permutation(np.resize(levels, k // 32))).repeat(32)
    a = np.empty((k // 512, 16))
    for p in range(k // 512):
        a[p, :8] = np.random.permutation(np.resize(levels, 8))
        for g in range(8):
            far = levels[np.abs(levels - a[p, g]) >= 10]
            a[p, g + 8] = far[np.random.randint(len(far))]
    return np.exp2(a.ravel()).repeat(32)


def f64(x):
    return np.asarray(x).astype(np.float64)


def striped8(idx):
    return np.concatenate([x.reshape(-1, 16).T for x in idx]).astype(np.uint16)


def runs(offs, k):
    lists = np.stack([offs[16 * r : 16 * r + 16].T.reshape(-1) for r in range(8)]).astype(np.int64)
    return lists[np.arange(k) % 512 // 64]


def pack_weight(w):
    k, n = w.shape
    w = f64(np.asarray(w, np.float32).astype(ml_dtypes.bfloat16)).reshape(k // 32, 32, n)
    amax = np.abs(w).max(1)
    byte = np.clip(np.where(amax > 0, np.frexp(amax)[1] - 1 + 127 - 7, 1), 1, 254)
    scaled = (w * np.exp2(127.0 - byte)[:, None, :]).reshape(k, n).astype(np.float32)
    words = np.ascontiguousarray(scaled.reshape(k // 512, 128, 4, n).transpose(0, 1, 3, 2)).astype(ml_dtypes.float8_e4m3fn).view(np.uint8)
    return words, np.ascontiguousarray(byte.astype(np.uint8).reshape(k // 512, 16, n))


def unpack_weight(words, scales):
    g, p, n, _ = words.shape
    vals = np.ascontiguousarray(words).view(ml_dtypes.float8_e4m3fn).astype(np.float64) * np.repeat(np.exp2(scales.astype(np.float64) - 127.0), 8, axis=1)[..., None]
    return vals.transpose(0, 1, 3, 2).reshape(g * 512, n)


E2M1 = np.array([0.0, 0.5, 1.0, 1.5, 2.0, 3.0, 4.0, 6.0, -0.0, -0.5, -1.0, -1.5, -2.0, -3.0, -4.0, -6.0])


def pack_fp4(w):
    k, n = w.shape
    w = f64(np.asarray(w, np.float32).astype(ml_dtypes.bfloat16)).reshape(k // 32, 32, n)
    amax = np.abs(w).max(1)
    mant, ex = np.frexp(amax / 6.0)
    byte = np.clip(np.where(amax > 0, np.where(mant > 0.5, ex, ex - 1) + 127, 1), 1, 254)
    scaled = (w * np.exp2(127.0 - byte)[:, None, :]).reshape(k, n).astype(np.float32)
    c = np.ascontiguousarray(scaled.reshape(k // 512, 128, 4, n).transpose(0, 1, 3, 2)).astype(ml_dtypes.float4_e2m1fn).view(np.uint8) & 0xF
    words = (c[..., 0::2] | (c[..., 1::2] << 4)).reshape(k // 512, 128, 2 * n)
    return np.ascontiguousarray(words), np.ascontiguousarray(byte.astype(np.uint8).reshape(k // 512, 16, n))


def unpack_fp4(words, scales):
    g, _, n = scales.shape
    words = np.ascontiguousarray(words).reshape(g, 128, n, 2)
    nib = np.empty((g, 128, n, 4), np.uint8)
    nib[..., 0::2] = words & 0xF
    nib[..., 1::2] = words >> 4
    vals = E2M1[nib] * np.repeat(np.exp2(scales.astype(np.float64) - 127.0), 8, axis=1)[..., None]
    return vals.transpose(0, 1, 3, 2).reshape(g * 512, n)


K, T, S, H, W, G, U = 512, 1024, 512, 512, 256, 2048, 1024


def setup_inputs():
    n = np.random.standard_normal
    s = mx_kscale(K)[:, None]
    packed_xT = pack_weight(n((K, T)) * s)
    packed_w1 = pack_fp4(n((K, H)) / np.sqrt(K) / s)
    packed_dT = pack_weight(n((K, G)) / s)
    perm = np.stack([np.random.permutation(S) for _ in range(8)])
    perm2 = np.stack([np.random.permutation(U) for _ in range(8)])
    return {
        "x_words": packed_xT[0],
        "x_scales": packed_xT[1],
        "w1_words": packed_w1[0],
        "w1_scales": packed_w1[1],
        "gs": (np.random.uniform(0.5, 1.5, (K, 1)) * s).astype(np.float32),
        "d_words": packed_dT[0],
        "d_scales": packed_dT[1],
        "offs": striped8(np.random.randint(0, T, (8, S))),
        "n1": striped8(perm[:, :W]),
        "n2": striped8(perm[:, W:]),
        "n3": striped8(np.stack([np.random.permutation(S) for _ in range(8)])),
        "k1": striped8(np.random.randint(0, G, (8, H))),
        "k2": striped8(np.random.randint(0, G, (8, H))),
        "hz": striped8(np.random.randint(0, T, (8, S))),
        "n4": striped8(perm2[:, :S]),
        "n5": striped8(perm2[:, S:]),
        "n6": striped8(np.stack([np.random.permutation(S) for _ in range(8)])),
    }


def reference(x_words, x_scales, w1_words, w1_scales, gs, d_words, d_scales, offs, n1, n2, n3, k1, k2, hz, n4, n5, n6):
    d_k1 = unpack_weight(d_words, d_scales)[np.arange(K)[:, None], runs(k1, K)]
    xq = unpack_weight(x_words, x_scales)[np.arange(K)[:, None], runs(offs, K)]
    y = unpack_fp4(w1_words, w1_scales).T @ xq
    pa = y[np.arange(H)[:, None], runs(n1, H)]
    pb = y[np.arange(H)[:, None], runs(n2, H)]
    rb = pa - pb
    ua = np.zeros((H, S))
    ua[np.arange(H)[:, None], runs(n1, H)] = pb
    ub = ua.copy()
    ub[np.arange(H)[:, None], runs(n2, H)] = rb
    z = f64(gs) * (np.maximum(ub, 0.5 * (ub[np.arange(H)[:, None], runs(n3, H)])))
    d_k2 = unpack_weight(d_words, d_scales)[np.arange(K)[:, None], runs(k2, K)]
    x_hz = unpack_weight(x_words, x_scales)[np.arange(K)[:, None], runs(hz, K)]
    h2 = 0.0625 * ((d_k1.T @ mxq(z, 0, "e4m3") + d_k2.T @ x_hz))
    ds = np.zeros((H, S))
    ds[np.arange(H)[:, None], runs(n6, H)] = h2
    up = np.maximum(h2, ds)
    ph = np.zeros((H, U))
    ph[np.arange(H)[:, None], runs(n4, H)] = ds
    out = ph.copy()
    out[np.arange(H)[:, None], runs(n5, H)] = up
    return out

@@ -1,0 +1,293 @@
+from contextlib import ExitStack
+
+import concourse.mybir as mybir
+
+FLOPS = 805306368
+
+F32 = mybir.dt.float32
+BF16 = mybir.dt.bfloat16
+I32 = mybir.dt.int32
+U32 = mybir.dt.uint32
+U16 = mybir.dt.uint16
+U8 = mybir.dt.uint8
+FP8X4 = mybir.dt.float8_e4m3fn_x4
+FP4X4 = mybir.dt.float4_e2m1fn_x4
+ALU = mybir.AluOpType
+COPY = mybir.ActivationFunctionType.Copy
+
+P = 128
+PACK = 4
+S = 512
+HALF = 256
+PAGE = 1024
+T = 1024
+G = 2048
+NQ = 4
+QW = S // NQ
+LAST = PACK - 1
+
+
+def tile_picked_dhzmhswapdpagsn_none_p_kernel(
+    tc, x_words, x_scales, w1_words, w1_scales, gs, d_words, d_scales, offs, n1, n2, n3, k1, k2, hz, n4, n5, n6, out
+):
+    nc = tc.nc
+    with ExitStack() as ctx:
+        held = ctx.enter_context(tc.tile_pool(name="lists", bufs=1))
+        pool = ctx.enter_context(tc.tile_pool(name="work", bufs=1))
+        psum = ctx.enter_context(tc.psum_pool(name="psum", bufs=8))
+
+        def sb(name, width, dtype, tag=None):
+            return pool.tile([P, width], dtype, name=name, tag=tag or name, align_bytes=64)
+
+        def load_list(name, src):
+            tile = held.tile(list(src.shape), U16, name=name)
+            nc.sync.dma_start(tile[:], src)
+            return tile
+
+        def entries(lst, first, count):
+            return lst[:, first // 16 : (first + count) // 16]
+
+        def zeroed_bytes(engine, name, width):
+            tile = sb(name, width, U8)
+            engine.memset(tile[:].bitcast(I32), 0)
+            return tile
+
+        def place_rows(plane, picked):
+            for i in range(4):
+                nc.sync.dma_start(plane[:].bitcast(I32)[i:P:32, :], picked[:].bitcast(I32)[8 * i : P : 32, :])
+
+        def deal(engine_copy, dst, src, run):
+            engine_copy(
+                dst.rearrange("p (t c i) -> p c t i", t=PACK, i=run),
+                src.rearrange("p (c i t) -> p c t i", t=PACK, i=run),
+            )
+
+        x_byte_table = zeroed_bytes(nc.gpsimd, "x_byte_table", T)
+        w1_raw_plane = zeroed_bytes(nc.gpsimd, "w1_raw_plane", S)
+        d_byte_table = zeroed_bytes(nc.vector, "d_byte_table", G)
+        xq_plane = zeroed_bytes(nc.vector, "xq_plane", S)
+        xh_plane = zeroed_bytes(nc.vector, "xh_plane", S)
+        dk_planes = zeroed_bytes(nc.vector, "dk_planes", 2 * S)
+
+        offs_l = load_list("offs_l", offs)
+        nc.sync.dma_start(x_byte_table[:].bitcast(I32)[0:P:8, :], x_scales[0].bitcast(I32))
+        x_word_table = sb("x_word_table", T, U32)
+        nc.sync.dma_start(x_word_table[:].bitcast(I32), x_words[0].rearrange("p n t -> p (n t)").bitcast(I32))
+        w1_raw = sb("w1_raw", 2 * S, U8)
+        nc.sync.dma_start(w1_raw[:].bitcast(I32), w1_words[0].bitcast(I32))
+        for q in range(4):
+            nc.sync.dma_start(
+                w1_raw_plane[:].bitcast(I32)[32 * q : 32 * q + 4, :], w1_scales[0, 4 * q : 4 * q + 4, :].bitcast(I32)
+            )
+        hz_l = load_list("hz_l", hz)
+        nc.sync.dma_start(d_byte_table[:].bitcast(I32)[0:P:8, :], d_scales[0].bitcast(I32))
+        k1_l = load_list("k1_l", k1)
+        k2_l = load_list("k2_l", k2)
+
+        xq_bytes = sb("xq_bytes", S, U8)
+        nc.vector.tensor_copy(xq_bytes[:], x_byte_table[:].indirect(offs_l[:]))
+        place_rows(xq_plane, xq_bytes)
+        xq_words = sb("xq_words", S, U32)
+        nc.vector.tensor_copy(xq_words[:], x_word_table[:].indirect(offs_l[:]))
+        w1_dealt = sb("w1_dealt", 2 * S, U8)
+        deal(nc.scalar.copy, w1_dealt[:].bitcast(U16), w1_raw[:].bitcast(U16), 8)
+        w1_plane = sb("w1_plane", S, U8)
+        deal(nc.vector.tensor_copy, w1_plane[:], w1_raw_plane[:], 16)
+
+        n2_l = load_list("n2_l", n2)
+        n1_l = load_list("n1_l", n1)
+        n3_l = load_list("n3_l", n3)
+        gs_sb = sb("gs_sb", PACK, F32)
+        nc.sync.dma_start(gs_sb[:], gs.rearrange("(p t) o -> p (t o)", t=PACK))
+        d_word_table = sb("d_word_table", G, U32)
+        nc.sync.dma_start(d_word_table[:].bitcast(I32), d_words[0].rearrange("p n t -> p (n t)").bitcast(I32))
+
+        xh_bytes = sb("xh_bytes", S, U8)
+        nc.vector.tensor_copy(xh_bytes[:], x_byte_table[:].indirect(hz_l[:]))
+        place_rows(xh_plane, xh_bytes)
+        dk_bytes = sb("dk_bytes", 2 * S, U8)
+        dk_bytes_dealt = sb("dk_bytes_dealt", 2 * S, U8)
+        for a, lst in enumerate((k1_l, k2_l)):
+            nc.vector.tensor_copy(dk_bytes[:, a * S : (a + 1) * S], d_byte_table[:].indirect(lst[:]))
+        for a in range(2):
+            deal(nc.vector.tensor_copy, dk_bytes_dealt[:, a * S : (a + 1) * S], dk_bytes[:, a * S : (a + 1) * S], 16)
+        place_rows(dk_planes, dk_bytes_dealt)
+
+        n6_l = load_list("n6_l", n6)
+        n4_l = load_list("n4_l", n4)
+        n5_l = load_list("n5_l", n5)
+
+        y_banks = []
+        for t in range(PACK):
+            bank = psum.tile([P, S], F32, name="bank", tag="bank")
+            nc.tensor.matmul_mx(
+                bank[:],
+                lhsT=w1_dealt[:, 2 * P * t : 2 * P * (t + 1)].bitcast(FP4X4),
+                lhsT_scale=w1_plane[:, P * t : P * (t + 1)],
+                rhs=xq_words[:].bitcast(FP8X4),
+                rhs_scale=xq_plane[:],
+                start=True,
+                stop=True,
+            )
+            y_banks.append(bank)
+
+        y, pa, pb, ub, larger = {}, {}, {}, {}, {}
+        z_bf = [sb("z_bf%d" % q, QW * PACK, BF16) for q in range(NQ)]
+        z_words = sb("z_words", S, U32)
+        z_plane = sb("z_plane", S, U8)
+
+        def put_pb(t):
+            y[t] = sb("y%d" % t, S, F32)
+            nc.scalar.copy(y[t][:], y_banks[t][:])
+            pb[t] = sb("pb%d" % t, HALF, F32)
+            nc.scalar.activation(pb[t][:], y[t][:].indirect(n2_l[:]), COPY)
+            ub[t] = sb("ub%d" % t, S, F32)
+            nc.vector.tensor_copy(ub[t][:].indirect(n1_l[:]), pb[t][:])
+
+        def fetch_pa(t):
+            pa[t] = sb("pa%d" % t, HALF, F32)
+            nc.scalar.activation(pa[t][:], y[t][:].indirect(n1_l[:]), COPY)
+
+        def put_rb(t):
+            npb = sb("npb%d" % t, HALF, F32)
+            nc.scalar.mul(npb[:], pb[t][:], -1.0)
+            nc.vector.tensor_tensor(ub[t][:].indirect(n2_l[:]), pa[t][:], npb[:], ALU.add)
+
+        def take_larger(t):
+            fetched = sb("fetched%d" % t, S, F32)
+            for h in range(2):
+                nc.scalar.activation(
+                    fetched[:, h * HALF : (h + 1) * HALF], ub[t][:].indirect(entries(n3_l, h * HALF, HALF)), COPY
+                )
+            larger[t] = sb("larger%d" % t, S, F32)
+            nc.vector.scalar_tensor_tensor(larger[t][:], fetched[:], 0.5, ub[t][:], ALU.mult, ALU.max)
+
+        def weigh(t, q):
+            nc.scalar.activation(
+                z_bf[q][:].rearrange("p (j t) -> p t j", t=PACK)[:, t, :],
+                larger[t][:, q * QW : (q + 1) * QW],
+                COPY,
+                scale=gs_sb[:, t : t + 1],
+            )
+
+        def weigh_all(t):
+            for q in range(NQ):
+                weigh(t, q)
+
+        def pick_d_words(name, lst, tag):
+            picked = sb(name, S, U32, tag=tag)
+            nc.vector.tensor_copy(picked[:], d_word_table[:].indirect(lst[:]))
+            return picked
+
+        def deal_d_words(name, picked, tag):
+            dealt = sb(name, S, U32, tag=tag)
+            deal(nc.vector.tensor_copy, dealt[:].bitcast(I32), picked[:].bitcast(I32), 4)
+            return dealt
+
+        def pick_xh_words(h, tag):
+            picked = sb("xh_words%d" % h, HALF, U32, tag=tag)
+            nc.vector.tensor_copy(picked[:], x_word_table[:].indirect(entries(hz_l, h * HALF, HALF)))
+            return picked
+
+        put_pb(0)
+        put_pb(1)
+        fetch_pa(0)
+        put_rb(0)
+        fetch_pa(1)
+        put_rb(1)
+        put_pb(2)
+        take_larger(0)
+        fetch_pa(2)
+        put_rb(2)
+        dk1_picked = pick_d_words("dk1_picked", k1_l, "pb2")
+        take_larger(1)
+        put_pb(3)
+        weigh_all(0)
+        dk1_words = deal_d_words("dk1_words", dk1_picked, "larger0")
+        take_larger(2)
+        fetch_pa(3)
+        dk2_picked = pick_d_words("dk2_picked", k2_l, "y3")
+        put_rb(3)
+        dk2_words = deal_d_words("dk2_words", dk2_picked, "pb3")
+        weigh_all(1)
+        xh_words = [pick_xh_words(0, "larger1")]
+        weigh_all(2)
+        xh_words.append(pick_xh_words(1, "larger2"))
+
+        h2 = [sb("h2_%d" % t, S, F32) for t in range(PACK)]
+        ds = [sb("ds%d" % t, PAGE, F32) for t in range(PACK)]
+
+        def second_product(dst, t, q):
+            rows = slice(P * t, P * (t + 1))
+            cols = slice(QW * q, QW * (q + 1))
+            nc.tensor.matmul_mx(
+                dst,
+                lhsT=dk2_words[:, rows].bitcast(FP8X4),
+                lhsT_scale=dk_planes[:, S + P * t : S + P * (t + 1)],
+                rhs=xh_words[q // 2][:, QW * (q % 2) : QW * (q % 2 + 1)].bitcast(FP8X4),
+                rhs_scale=xh_plane[:, cols],
+                start=True,
+                stop=False,
+            )
+            nc.tensor.matmul_mx(
+                dst,
+                lhsT=dk1_words[:, rows].bitcast(FP8X4),
+                lhsT_scale=dk_planes[:, rows],
+                rhs=z_words[:, cols].bitcast(FP8X4),
+                rhs_scale=z_plane[:, cols],
+                start=False,
+                stop=True,
+            )
+
+        fetched = sb("fetched%d" % LAST, S, F32)
+        larger[LAST] = sb("larger%d" % LAST, S, F32)
+        for q in range(NQ):
+            cols = slice(QW * q, QW * (q + 1))
+            nc.scalar.activation(fetched[:, cols], ub[LAST][:].indirect(entries(n3_l, q * QW, QW)), COPY)
+            nc.vector.scalar_tensor_tensor(
+                larger[LAST][:, cols], fetched[:, cols], 0.5, ub[LAST][:, cols], ALU.mult, ALU.max
+            )
+        for q in range(NQ):
+            cols = slice(QW * q, QW * (q + 1))
+            weigh(LAST, q)
+            nc.vector.quantize_mx(z_words[:, cols].bitcast(FP8X4), z_plane[:, cols], z_bf[q][:])
+        for q in range(NQ):
+            cols = slice(QW * q, QW * (q + 1))
+            bank = psum.tile([P, S], F32, name="bank", tag="bank")
+            second_product(bank[:, 0:QW], 0, q)
+            nc.scalar.mul(h2[0][:, cols], bank[:, 0:QW], 0.0625)
+            nc.vector.tensor_copy(ds[0][:].indirect(entries(n6_l, q * QW, QW)), h2[0][:, cols])
+
+        for t in range(1, PACK):
+            bank = psum.tile([P, S], F32, name="bank", tag="bank")
+            for q in range(NQ):
+                second_product(bank[:, QW * q : QW * (q + 1)], t, q)
+            nc.scalar.mul(h2[t][:], bank[:], 0.0625)
+
+        up, page = {}, {}
+        out_rows = out.rearrange("(p t) w -> t p w", t=PACK)
+
+        def send(t):
+            nc.vector.tensor_copy(ds[t][:].indirect(n6_l[:]), h2[t][:])
+
+        def put_ds(t):
+            up[t] = sb("up%d" % t, S, F32, tag="larger2" if t == 0 else None)
+            nc.vector.tensor_tensor(up[t][:], h2[t][:], ds[t][:, 0:S], ALU.max)
+            page[t] = sb("page%d" % t, PAGE, F32, tag="larger0" if t == 0 else None)
+            nc.vector.tensor_copy(page[t][:].indirect(n4_l[:]), ds[t][:, 0:S])
+
+        def put_up(t):
+            nc.vector.tensor_copy(page[t][:].indirect(n5_l[:]), up[t][:])
+            nc.sync.dma_start(out_rows[t], page[t][:])
+
+        send(1)
+        put_ds(0)
+        send(2)
+        put_up(0)
+        put_ds(1)
+        send(3)
+        put_up(1)
+        put_ds(2)
+        put_ds(3)
+        put_up(2)
+        put_up(3)

@@ -1,6 +1,7 @@
 from contextlib import ExitStack
 
 import concourse.mybir as mybir
+from concourse.masks import make_identity
 
 FLOPS = 805306368
 
@@ -14,6 +15,7 @@ FP8X4 = mybir.dt.float8_e4m3fn_x4
 FP4X4 = mybir.dt.float4_e2m1fn_x4
 ALU = mybir.AluOpType
 COPY = mybir.ActivationFunctionType.Copy
+RELU = mybir.ActivationFunctionType.Relu
 
 P = 128
 PACK = 4
@@ -52,9 +54,11 @@ def tile_picked_dhzmhswapdpagsn_none_p_kernel(
             engine.memset(tile[:].bitcast(I32), 0)
             return tile
 
-        def place_rows(plane, picked):
+        def place_rows(plane, picked, first=0):
             for i in range(4):
-                nc.sync.dma_start(plane[:].bitcast(I32)[i:P:32, :], picked[:].bitcast(I32)[8 * i : P : 32, :])
+                nc.sync.dma_start(
+                    plane[:].bitcast(I32)[first + i : P : 32, :], picked[:].bitcast(I32)[8 * i : P : 32, :]
+                )
 
         def deal(engine_copy, dst, src, run):
             engine_copy(
@@ -68,6 +72,10 @@ def tile_picked_dhzmhswapdpagsn_none_p_kernel(
         xq_plane = zeroed_bytes(nc.vector, "xq_plane", S)
         xh_plane = zeroed_bytes(nc.vector, "xh_plane", S)
         dk_planes = zeroed_bytes(nc.vector, "dk_planes", 2 * S)
+        minus_one = sb("minus_one", HALF, F32)
+        nc.vector.memset(minus_one[:], -1.0)
+        identity = sb("identity", P, F32)
+        make_identity(nc, identity[:])
 
         offs_l = load_list("offs_l", offs)
         nc.sync.dma_start(x_byte_table[:].bitcast(I32)[0:P:8, :], x_scales[0].bitcast(I32))
@@ -136,22 +144,22 @@ def tile_picked_dhzmhswapdpagsn_none_p_kernel(
         z_words = sb("z_words", S, U32)
         z_plane = sb("z_plane", S, U8)
 
-        def put_pb(t):
+        def drain_y(t):
             y[t] = sb("y%d" % t, S, F32)
             nc.scalar.copy(y[t][:], y_banks[t][:])
+
+        def put_pb(t):
             pb[t] = sb("pb%d" % t, HALF, F32)
-            nc.scalar.activation(pb[t][:], y[t][:].indirect(n2_l[:]), COPY)
+            nc.scalar.activation(pb[t][:], y[t][:].indirect(n2_l[:]), COPY, scale=-1.0)
             ub[t] = sb("ub%d" % t, S, F32)
-            nc.vector.tensor_copy(ub[t][:].indirect(n1_l[:]), pb[t][:])
+            nc.vector.tensor_tensor(ub[t][:].indirect(n1_l[:]), pb[t][:], minus_one[:], ALU.mult)
 
         def fetch_pa(t):
             pa[t] = sb("pa%d" % t, HALF, F32)
             nc.scalar.activation(pa[t][:], y[t][:].indirect(n1_l[:]), COPY)
 
         def put_rb(t):
-            npb = sb("npb%d" % t, HALF, F32)
-            nc.scalar.mul(npb[:], pb[t][:], -1.0)
-            nc.vector.tensor_tensor(ub[t][:].indirect(n2_l[:]), pa[t][:], npb[:], ALU.add)
+            nc.vector.tensor_tensor(ub[t][:].indirect(n2_l[:]), pa[t][:], pb[t][:], ALU.add)
 
         def take_larger(t):
             fetched = sb("fetched%d" % t, S, F32)
@@ -162,17 +170,17 @@ def tile_picked_dhzmhswapdpagsn_none_p_kernel(
             larger[t] = sb("larger%d" % t, S, F32)
             nc.vector.scalar_tensor_tensor(larger[t][:], fetched[:], 0.5, ub[t][:], ALU.mult, ALU.max)
 
-        def weigh(t, q):
+        pairs = sb("pairs", PACK * S, BF16)
+        pair_slots = pairs[:].rearrange("p (q u j e) -> p u e q j", q=NQ, u=2, e=2)
+        pair_words = pairs[:].bitcast(F32).rearrange("p (q u j) -> p q j u", q=NQ, u=2)
+
+        def weigh_all(t):
             nc.scalar.activation(
-                z_bf[q][:].rearrange("p (j t) -> p t j", t=PACK)[:, t, :],
-                larger[t][:, q * QW : (q + 1) * QW],
+                pair_slots[:, t // 2, t % 2, :, :],
+                larger[t][:].rearrange("p (q j) -> p q j", q=NQ),
                 COPY,
                 scale=gs_sb[:, t : t + 1],
             )
-
-        def weigh_all(t):
-            for q in range(NQ):
-                weigh(t, q)
 
         def pick_d_words(name, lst, tag):
             picked = sb(name, S, U32, tag=tag)
@@ -184,51 +192,55 @@ def tile_picked_dhzmhswapdpagsn_none_p_kernel(
             deal(nc.vector.tensor_copy, dealt[:].bitcast(I32), picked[:].bitcast(I32), 4)
             return dealt
 
-        def pick_xh_words(h, tag):
-            picked = sb("xh_words%d" % h, HALF, U32, tag=tag)
-            nc.vector.tensor_copy(picked[:], x_word_table[:].indirect(entries(hz_l, h * HALF, HALF)))
+        def pick_xh_words(q, tag):
+            picked = sb("xh_words%d" % q, QW, U32, tag=tag)
+            nc.vector.tensor_copy(picked[:], x_word_table[:].indirect(entries(hz_l, q * QW, QW)))
             return picked
 
+        drain_y(0)
         put_pb(0)
+        drain_y(1)
         put_pb(1)
         fetch_pa(0)
         put_rb(0)
         fetch_pa(1)
         put_rb(1)
+        drain_y(2)
         put_pb(2)
+        drain_y(3)
         take_larger(0)
         fetch_pa(2)
         put_rb(2)
-        dk1_picked = pick_d_words("dk1_picked", k1_l, "pb2")
+        dk1_picked = pick_d_words("dk1_picked", k1_l, "y2")
         take_larger(1)
         put_pb(3)
         weigh_all(0)
         dk1_words = deal_d_words("dk1_words", dk1_picked, "larger0")
         take_larger(2)
         fetch_pa(3)
-        dk2_picked = pick_d_words("dk2_picked", k2_l, "y3")
         put_rb(3)
-        dk2_words = deal_d_words("dk2_words", dk2_picked, "pb3")
+        dk2_picked = pick_d_words("dk2_picked", k2_l, "y3")
         weigh_all(1)
-        xh_words = [pick_xh_words(0, "larger1")]
         weigh_all(2)
-        xh_words.append(pick_xh_words(1, "larger2"))
 
         h2 = [sb("h2_%d" % t, S, F32) for t in range(PACK)]
         ds = [sb("ds%d" % t, PAGE, F32) for t in range(PACK)]
 
-        def second_product(dst, t, q):
+        def hashed_pass(dst, t, q, start):
             rows = slice(P * t, P * (t + 1))
             cols = slice(QW * q, QW * (q + 1))
             nc.tensor.matmul_mx(
                 dst,
                 lhsT=dk2_words[:, rows].bitcast(FP8X4),
                 lhsT_scale=dk_planes[:, S + P * t : S + P * (t + 1)],
-                rhs=xh_words[q // 2][:, QW * (q % 2) : QW * (q % 2 + 1)].bitcast(FP8X4),
+                rhs=xh_words[q][:].bitcast(FP8X4),
                 rhs_scale=xh_plane[:, cols],
-                start=True,
+                start=start,
                 stop=False,
             )
+
+        def z_pass(dst, t, cols):
+            rows = slice(P * t, P * (t + 1))
             nc.tensor.matmul_mx(
                 dst,
                 lhsT=dk1_words[:, rows].bitcast(FP8X4),
@@ -239,53 +251,96 @@ def tile_picked_dhzmhswapdpagsn_none_p_kernel(
                 stop=True,
             )
 
-        fetched = sb("fetched%d" % LAST, S, F32)
-        larger[LAST] = sb("larger%d" % LAST, S, F32)
-        for q in range(NQ):
+        last_larger = {}
+
+        def last_larger_quarter(q):
             cols = slice(QW * q, QW * (q + 1))
-            nc.scalar.activation(fetched[:, cols], ub[LAST][:].indirect(entries(n3_l, q * QW, QW)), COPY)
-            nc.vector.scalar_tensor_tensor(
-                larger[LAST][:, cols], fetched[:, cols], 0.5, ub[LAST][:, cols], ALU.mult, ALU.max
-            )
-        for q in range(NQ):
+            fetched = sb("last_fetched%d" % q, QW, F32)
+            nc.scalar.activation(fetched[:], ub[LAST][:].indirect(entries(n3_l, q * QW, QW)), COPY)
+            last_larger[q] = sb("last_larger%d" % q, QW, F32)
+            nc.vector.scalar_tensor_tensor(last_larger[q][:], fetched[:], 0.5, ub[LAST][:, cols], ALU.mult, ALU.max)
+
+        def quantise_quarter(q):
             cols = slice(QW * q, QW * (q + 1))
-            weigh(LAST, q)
             nc.vector.quantize_mx(z_words[:, cols].bitcast(FP8X4), z_plane[:, cols], z_bf[q][:])
-        for q in range(NQ):
+
+        def weave_quarter(q):
+            nc.scalar.activation(
+                pair_slots[:, LAST // 2, LAST % 2, q, :], last_larger[q][:], COPY, scale=gs_sb[:, LAST : LAST + 1]
+            )
+            nc.vector.tensor_copy(z_bf[q][:].bitcast(F32).rearrange("p (j u) -> p j u", u=2), pair_words[:, q, :, :])
+
+        def send_first_quarter(q):
             cols = slice(QW * q, QW * (q + 1))
             bank = psum.tile([P, S], F32, name="bank", tag="bank")
-            second_product(bank[:, 0:QW], 0, q)
+            hashed_pass(bank[:, 0:QW], 0, q, True)
+            z_pass(bank[:, 0:QW], 0, cols)
             nc.scalar.mul(h2[0][:, cols], bank[:, 0:QW], 0.0625)
             nc.vector.tensor_copy(ds[0][:].indirect(entries(n6_l, q * QW, QW)), h2[0][:, cols])
+
+        for q in range(NQ):
+            last_larger_quarter(q)
+        weave_quarter(0)
+        for q in range(NQ):
+            if q + 1 < NQ:
+                weave_quarter(q + 1)
+            quantise_quarter(q)
+        dk2_words = deal_d_words("dk2_words", dk2_picked, "last_fetched0")
+        xh_words = [
+            pick_xh_words(q, tag)
+            for q, tag in enumerate(("last_fetched1", "last_fetched2", "last_fetched3", "last_larger0"))
+        ]
+        for q in range(NQ):
+            send_first_quarter(q)
 
         for t in range(1, PACK):
             bank = psum.tile([P, S], F32, name="bank", tag="bank")
             for q in range(NQ):
-                second_product(bank[:, QW * q : QW * (q + 1)], t, q)
+                hashed_pass(bank[:, QW * q : QW * (q + 1)], t, q, q == 0)
+            z_pass(bank[:], t, slice(0, S))
             nc.scalar.mul(h2[t][:], bank[:], 0.0625)
 
-        up, page = {}, {}
+        excess, page = {}, {}
         out_rows = out.rearrange("(p t) w -> t p w", t=PACK)
 
         def send(t):
             nc.vector.tensor_copy(ds[t][:].indirect(n6_l[:]), h2[t][:])
 
         def put_ds(t):
-            up[t] = sb("up%d" % t, S, F32, tag="larger2" if t == 0 else None)
-            nc.vector.tensor_tensor(up[t][:], h2[t][:], ds[t][:, 0:S], ALU.max)
             page[t] = sb("page%d" % t, PAGE, F32, tag="larger0" if t == 0 else None)
             nc.vector.tensor_copy(page[t][:].indirect(n4_l[:]), ds[t][:, 0:S])
 
+        def find_excess(t):
+            minus_h2 = sb("minus_h2_%d" % t, S, F32)
+            nc.scalar.mul(minus_h2[:], h2[t][:], -1.0)
+            turned = psum.tile([P, S], F32, name="bank", tag="bank")
+            for c in range(S // P):
+                cols = slice(P * c, P * (c + 1))
+                nc.tensor.matmul(turned[:, cols], minus_h2[:, cols], identity[:], start=True, stop=False, is_transpose=True)
+                nc.tensor.matmul(turned[:, cols], ds[t][:, cols], identity[:], start=False, stop=True, is_transpose=True)
+            clipped = sb("clipped%d" % t, S, F32)
+            nc.scalar.activation(clipped[:], turned[:], RELU)
+            back = psum.tile([P, S], F32, name="bank", tag="bank")
+            for c in range(S // P):
+                cols = slice(P * c, P * (c + 1))
+                nc.tensor.transpose(back[:, cols], clipped[:, cols], identity[:])
+            excess[t] = sb("excess%d" % t, S, F32)
+            nc.scalar.copy(excess[t][:], back[:])
+
         def put_up(t):
-            nc.vector.tensor_copy(page[t][:].indirect(n5_l[:]), up[t][:])
+            nc.vector.tensor_tensor(page[t][:].indirect(n5_l[:]), h2[t][:], excess[t][:], ALU.add)
             nc.sync.dma_start(out_rows[t], page[t][:])
 
+        find_excess(0)
         send(1)
+        find_excess(1)
         put_ds(0)
         send(2)
+        find_excess(2)
         put_up(0)
         put_ds(1)
         send(3)
+        find_excess(3)
         put_up(1)
         put_ds(2)
         put_ds(3)

@@ -19,14 +19,21 @@ RELU = mybir.ActivationFunctionType.Relu
 
 P = 128
 PACK = 4
+LAST = PACK - 1
 S = 512
-HALF = 256
+HALF = S // 2
 PAGE = 1024
 T = 1024
 G = 2048
+QUADRANT = 32
+ROWS_PER_QUADRANT = 4
+TABLE_ROW_STEP = 8
+LIST_GROUP = 16
+LINE = 16
+PSUM_BANKS = 8
 NQ = 4
 QW = S // NQ
-LAST = PACK - 1
+H2_FACTOR = 0.0625
 
 
 def tile_picked_dhzmhswapdpagsn_none_p_kernel(
@@ -36,10 +43,13 @@ def tile_picked_dhzmhswapdpagsn_none_p_kernel(
     with ExitStack() as ctx:
         held = ctx.enter_context(tc.tile_pool(name="lists", bufs=1))
         pool = ctx.enter_context(tc.tile_pool(name="work", bufs=1))
-        psum = ctx.enter_context(tc.psum_pool(name="psum", bufs=8))
+        psum = ctx.enter_context(tc.psum_pool(name="psum", bufs=PSUM_BANKS))
 
-        def sb(name, width, dtype, tag=None):
-            return pool.tile([P, width], dtype, name=name, tag=tag or name, align_bytes=64)
+        def sb(name, width, dtype, after=None):
+            return pool.tile([P, width], dtype, name=name, tag=after or name, align_bytes=64)
+
+        def new_bank():
+            return psum.tile([P, S], F32, name="bank", tag="bank")
 
         def load_list(name, src):
             tile = held.tile(list(src.shape), U16, name=name)
@@ -47,20 +57,22 @@ def tile_picked_dhzmhswapdpagsn_none_p_kernel(
             return tile
 
         def entries(lst, first, count):
-            return lst[:, first // 16 : (first + count) // 16]
+            return lst[:, first // LIST_GROUP : (first + count) // LIST_GROUP]
 
         def zeroed_bytes(engine, name, width):
             tile = sb(name, width, U8)
             engine.memset(tile[:].bitcast(I32), 0)
             return tile
 
-        def place_rows(plane, picked, first=0):
-            for i in range(4):
+        def place_rows(plane, picked):
+            for i in range(ROWS_PER_QUADRANT):
                 nc.sync.dma_start(
-                    plane[:].bitcast(I32)[first + i : P : 32, :], picked[:].bitcast(I32)[8 * i : P : 32, :]
+                    plane[:].bitcast(I32)[i:P:QUADRANT, :],
+                    picked[:].bitcast(I32)[TABLE_ROW_STEP * i : P : QUADRANT, :],
                 )
 
-        def deal(engine_copy, dst, src, run):
+        def deal(engine_copy, dst, src, element_bytes):
+            run = LINE // element_bytes
             engine_copy(
                 dst.rearrange("p (t c i) -> p c t i", t=PACK, i=run),
                 src.rearrange("p (c i t) -> p c t i", t=PACK, i=run),
@@ -78,17 +90,18 @@ def tile_picked_dhzmhswapdpagsn_none_p_kernel(
         make_identity(nc, identity[:])
 
         offs_l = load_list("offs_l", offs)
-        nc.sync.dma_start(x_byte_table[:].bitcast(I32)[0:P:8, :], x_scales[0].bitcast(I32))
+        nc.sync.dma_start(x_byte_table[:].bitcast(I32)[0:P:TABLE_ROW_STEP, :], x_scales[0].bitcast(I32))
         x_word_table = sb("x_word_table", T, U32)
         nc.sync.dma_start(x_word_table[:].bitcast(I32), x_words[0].rearrange("p n t -> p (n t)").bitcast(I32))
         w1_raw = sb("w1_raw", 2 * S, U8)
         nc.sync.dma_start(w1_raw[:].bitcast(I32), w1_words[0].bitcast(I32))
-        for q in range(4):
+        for quad in range(P // QUADRANT):
             nc.sync.dma_start(
-                w1_raw_plane[:].bitcast(I32)[32 * q : 32 * q + 4, :], w1_scales[0, 4 * q : 4 * q + 4, :].bitcast(I32)
+                w1_raw_plane[:].bitcast(I32)[QUADRANT * quad : QUADRANT * quad + ROWS_PER_QUADRANT, :],
+                w1_scales[0, ROWS_PER_QUADRANT * quad : ROWS_PER_QUADRANT * (quad + 1), :].bitcast(I32),
             )
         hz_l = load_list("hz_l", hz)
-        nc.sync.dma_start(d_byte_table[:].bitcast(I32)[0:P:8, :], d_scales[0].bitcast(I32))
+        nc.sync.dma_start(d_byte_table[:].bitcast(I32)[0:P:TABLE_ROW_STEP, :], d_scales[0].bitcast(I32))
         k1_l = load_list("k1_l", k1)
         k2_l = load_list("k2_l", k2)
 
@@ -98,9 +111,9 @@ def tile_picked_dhzmhswapdpagsn_none_p_kernel(
         xq_words = sb("xq_words", S, U32)
         nc.vector.tensor_copy(xq_words[:], x_word_table[:].indirect(offs_l[:]))
         w1_dealt = sb("w1_dealt", 2 * S, U8)
-        deal(nc.scalar.copy, w1_dealt[:].bitcast(U16), w1_raw[:].bitcast(U16), 8)
+        deal(nc.scalar.copy, w1_dealt[:].bitcast(U16), w1_raw[:].bitcast(U16), 2)
         w1_plane = sb("w1_plane", S, U8)
-        deal(nc.vector.tensor_copy, w1_plane[:], w1_raw_plane[:], 16)
+        deal(nc.gpsimd.tensor_copy, w1_plane[:], w1_raw_plane[:], 1)
 
         n2_l = load_list("n2_l", n2)
         n1_l = load_list("n1_l", n1)
@@ -118,7 +131,7 @@ def tile_picked_dhzmhswapdpagsn_none_p_kernel(
         for a, lst in enumerate((k1_l, k2_l)):
             nc.vector.tensor_copy(dk_bytes[:, a * S : (a + 1) * S], d_byte_table[:].indirect(lst[:]))
         for a in range(2):
-            deal(nc.vector.tensor_copy, dk_bytes_dealt[:, a * S : (a + 1) * S], dk_bytes[:, a * S : (a + 1) * S], 16)
+            deal(nc.vector.tensor_copy, dk_bytes_dealt[:, a * S : (a + 1) * S], dk_bytes[:, a * S : (a + 1) * S], 1)
         place_rows(dk_planes, dk_bytes_dealt)
 
         n6_l = load_list("n6_l", n6)
@@ -127,7 +140,7 @@ def tile_picked_dhzmhswapdpagsn_none_p_kernel(
 
         y_banks = []
         for t in range(PACK):
-            bank = psum.tile([P, S], F32, name="bank", tag="bank")
+            bank = new_bank()
             nc.tensor.matmul_mx(
                 bank[:],
                 lhsT=w1_dealt[:, 2 * P * t : 2 * P * (t + 1)].bitcast(FP4X4),
@@ -139,7 +152,7 @@ def tile_picked_dhzmhswapdpagsn_none_p_kernel(
             )
             y_banks.append(bank)
 
-        y, pa, pb, ub, larger = {}, {}, {}, {}, {}
+        y, pa, minus_pb, ub, larger = {}, {}, {}, {}, {}
         z_bf = [sb("z_bf%d" % q, QW * PACK, BF16) for q in range(NQ)]
         z_words = sb("z_words", S, U32)
         z_plane = sb("z_plane", S, U8)
@@ -149,17 +162,15 @@ def tile_picked_dhzmhswapdpagsn_none_p_kernel(
             nc.scalar.copy(y[t][:], y_banks[t][:])
 
         def put_pb(t):
-            pb[t] = sb("pb%d" % t, HALF, F32)
-            nc.scalar.activation(pb[t][:], y[t][:].indirect(n2_l[:]), COPY, scale=-1.0)
+            minus_pb[t] = sb("pb%d" % t, HALF, F32)
+            nc.scalar.activation(minus_pb[t][:], y[t][:].indirect(n2_l[:]), COPY, scale=-1.0)
             ub[t] = sb("ub%d" % t, S, F32)
-            nc.vector.tensor_tensor(ub[t][:].indirect(n1_l[:]), pb[t][:], minus_one[:], ALU.mult)
-
-        def fetch_pa(t):
-            pa[t] = sb("pa%d" % t, HALF, F32)
-            nc.scalar.activation(pa[t][:], y[t][:].indirect(n1_l[:]), COPY)
+            nc.vector.tensor_tensor(ub[t][:].indirect(n1_l[:]), minus_pb[t][:], minus_one[:], ALU.mult)
 
         def put_rb(t):
-            nc.vector.tensor_tensor(ub[t][:].indirect(n2_l[:]), pa[t][:], pb[t][:], ALU.add)
+            pa[t] = sb("pa%d" % t, HALF, F32)
+            nc.scalar.activation(pa[t][:], y[t][:].indirect(n1_l[:]), COPY)
+            nc.vector.tensor_tensor(ub[t][:].indirect(n2_l[:]), pa[t][:], minus_pb[t][:], ALU.add)
 
         def take_larger(t):
             fetched = sb("fetched%d" % t, S, F32)
@@ -171,29 +182,29 @@ def tile_picked_dhzmhswapdpagsn_none_p_kernel(
             nc.vector.scalar_tensor_tensor(larger[t][:], fetched[:], 0.5, ub[t][:], ALU.mult, ALU.max)
 
         pairs = sb("pairs", PACK * S, BF16)
-        pair_slots = pairs[:].rearrange("p (q u j e) -> p u e q j", q=NQ, u=2, e=2)
-        pair_words = pairs[:].bitcast(F32).rearrange("p (q u j) -> p q j u", q=NQ, u=2)
+        pair_halves = pairs[:].rearrange("p (q u j e) -> p u e q j", q=NQ, u=2, e=2)
+        whole_pairs = pairs[:].bitcast(F32).rearrange("p (q u j) -> p q j u", q=NQ, u=2)
 
-        def weigh_all(t):
+        def weigh(t):
             nc.scalar.activation(
-                pair_slots[:, t // 2, t % 2, :, :],
+                pair_halves[:, t // 2, t % 2, :, :],
                 larger[t][:].rearrange("p (q j) -> p q j", q=NQ),
                 COPY,
                 scale=gs_sb[:, t : t + 1],
             )
 
-        def pick_d_words(name, lst, tag):
-            picked = sb(name, S, U32, tag=tag)
+        def pick_d_words(name, lst, after):
+            picked = sb(name, S, U32, after)
             nc.vector.tensor_copy(picked[:], d_word_table[:].indirect(lst[:]))
             return picked
 
-        def deal_d_words(name, picked, tag):
-            dealt = sb(name, S, U32, tag=tag)
+        def deal_d_words(name, picked, after):
+            dealt = sb(name, S, U32, after)
             deal(nc.vector.tensor_copy, dealt[:].bitcast(I32), picked[:].bitcast(I32), 4)
             return dealt
 
-        def pick_xh_words(q, tag):
-            picked = sb("xh_words%d" % q, QW, U32, tag=tag)
+        def pick_xh_words(q, after):
+            picked = sb("xh_words%d" % q, QW, U32, after)
             nc.vector.tensor_copy(picked[:], x_word_table[:].indirect(entries(hz_l, q * QW, QW)))
             return picked
 
@@ -201,27 +212,23 @@ def tile_picked_dhzmhswapdpagsn_none_p_kernel(
         put_pb(0)
         drain_y(1)
         put_pb(1)
-        fetch_pa(0)
         put_rb(0)
-        fetch_pa(1)
         put_rb(1)
         drain_y(2)
         put_pb(2)
         drain_y(3)
         take_larger(0)
-        fetch_pa(2)
         put_rb(2)
-        dk1_picked = pick_d_words("dk1_picked", k1_l, "y2")
+        dk1_picked = pick_d_words("dk1_picked", k1_l, after="y2")
         take_larger(1)
         put_pb(3)
-        weigh_all(0)
-        dk1_words = deal_d_words("dk1_words", dk1_picked, "larger0")
+        weigh(0)
+        dk1_words = deal_d_words("dk1_words", dk1_picked, after="larger0")
         take_larger(2)
-        fetch_pa(3)
         put_rb(3)
-        dk2_picked = pick_d_words("dk2_picked", k2_l, "y3")
-        weigh_all(1)
-        weigh_all(2)
+        dk2_picked = pick_d_words("dk2_picked", k2_l, after="y3")
+        weigh(1)
+        weigh(2)
 
         h2 = [sb("h2_%d" % t, S, F32) for t in range(PACK)]
         ds = [sb("ds%d" % t, PAGE, F32) for t in range(PACK)]
@@ -253,52 +260,52 @@ def tile_picked_dhzmhswapdpagsn_none_p_kernel(
 
         last_larger = {}
 
-        def last_larger_quarter(q):
+        def take_last_larger(q):
             cols = slice(QW * q, QW * (q + 1))
             fetched = sb("last_fetched%d" % q, QW, F32)
             nc.scalar.activation(fetched[:], ub[LAST][:].indirect(entries(n3_l, q * QW, QW)), COPY)
             last_larger[q] = sb("last_larger%d" % q, QW, F32)
             nc.vector.scalar_tensor_tensor(last_larger[q][:], fetched[:], 0.5, ub[LAST][:, cols], ALU.mult, ALU.max)
 
-        def quantise_quarter(q):
+        def weigh_last_and_weave(q):
+            nc.scalar.activation(
+                pair_halves[:, LAST // 2, LAST % 2, q, :], last_larger[q][:], COPY, scale=gs_sb[:, LAST : LAST + 1]
+            )
+            nc.vector.tensor_copy(z_bf[q][:].bitcast(F32).rearrange("p (j u) -> p j u", u=2), whole_pairs[:, q, :, :])
+
+        def quantise(q):
             cols = slice(QW * q, QW * (q + 1))
             nc.vector.quantize_mx(z_words[:, cols].bitcast(FP8X4), z_plane[:, cols], z_bf[q][:])
 
-        def weave_quarter(q):
-            nc.scalar.activation(
-                pair_slots[:, LAST // 2, LAST % 2, q, :], last_larger[q][:], COPY, scale=gs_sb[:, LAST : LAST + 1]
-            )
-            nc.vector.tensor_copy(z_bf[q][:].bitcast(F32).rearrange("p (j u) -> p j u", u=2), pair_words[:, q, :, :])
-
-        def send_first_quarter(q):
+        def send_first_tile(q):
             cols = slice(QW * q, QW * (q + 1))
-            bank = psum.tile([P, S], F32, name="bank", tag="bank")
+            bank = new_bank()
             hashed_pass(bank[:, 0:QW], 0, q, True)
             z_pass(bank[:, 0:QW], 0, cols)
-            nc.scalar.mul(h2[0][:, cols], bank[:, 0:QW], 0.0625)
+            nc.scalar.mul(h2[0][:, cols], bank[:, 0:QW], H2_FACTOR)
             nc.vector.tensor_copy(ds[0][:].indirect(entries(n6_l, q * QW, QW)), h2[0][:, cols])
 
         for q in range(NQ):
-            last_larger_quarter(q)
-        weave_quarter(0)
+            take_last_larger(q)
+        weigh_last_and_weave(0)
         for q in range(NQ):
             if q + 1 < NQ:
-                weave_quarter(q + 1)
-            quantise_quarter(q)
-        dk2_words = deal_d_words("dk2_words", dk2_picked, "last_fetched0")
+                weigh_last_and_weave(q + 1)
+            quantise(q)
+        dk2_words = deal_d_words("dk2_words", dk2_picked, after="last_fetched0")
         xh_words = [
-            pick_xh_words(q, tag)
-            for q, tag in enumerate(("last_fetched1", "last_fetched2", "last_fetched3", "last_larger0"))
+            pick_xh_words(q, after)
+            for q, after in enumerate(("last_fetched1", "last_fetched2", "last_fetched3", "last_larger0"))
         ]
         for q in range(NQ):
-            send_first_quarter(q)
+            send_first_tile(q)
 
         for t in range(1, PACK):
-            bank = psum.tile([P, S], F32, name="bank", tag="bank")
+            bank = new_bank()
             for q in range(NQ):
                 hashed_pass(bank[:, QW * q : QW * (q + 1)], t, q, q == 0)
             z_pass(bank[:], t, slice(0, S))
-            nc.scalar.mul(h2[t][:], bank[:], 0.0625)
+            nc.scalar.mul(h2[t][:], bank[:], H2_FACTOR)
 
         excess, page = {}, {}
         out_rows = out.rearrange("(p t) w -> t p w", t=PACK)
@@ -307,20 +314,22 @@ def tile_picked_dhzmhswapdpagsn_none_p_kernel(
             nc.vector.tensor_copy(ds[t][:].indirect(n6_l[:]), h2[t][:])
 
         def put_ds(t):
-            page[t] = sb("page%d" % t, PAGE, F32, tag="larger0" if t == 0 else None)
+            page[t] = sb("page%d" % t, PAGE, F32, after="larger0" if t == 0 else None)
             nc.vector.tensor_copy(page[t][:].indirect(n4_l[:]), ds[t][:, 0:S])
 
         def find_excess(t):
             minus_h2 = sb("minus_h2_%d" % t, S, F32)
             nc.scalar.mul(minus_h2[:], h2[t][:], -1.0)
-            turned = psum.tile([P, S], F32, name="bank", tag="bank")
+            turned = new_bank()
             for c in range(S // P):
                 cols = slice(P * c, P * (c + 1))
-                nc.tensor.matmul(turned[:, cols], minus_h2[:, cols], identity[:], start=True, stop=False, is_transpose=True)
-                nc.tensor.matmul(turned[:, cols], ds[t][:, cols], identity[:], start=False, stop=True, is_transpose=True)
+                for term, first in ((minus_h2, True), (ds[t], False)):
+                    nc.tensor.matmul(
+                        turned[:, cols], term[:, cols], identity[:], start=first, stop=not first, is_transpose=True
+                    )
             clipped = sb("clipped%d" % t, S, F32)
             nc.scalar.activation(clipped[:], turned[:], RELU)
-            back = psum.tile([P, S], F32, name="bank", tag="bank")
+            back = new_bank()
             for c in range(S // P):
                 cols = slice(P * c, P * (c + 1))
                 nc.tensor.transpose(back[:, cols], clipped[:, cols], identity[:])

from contextlib import ExitStack

import concourse.mybir as mybir
from concourse.masks import make_identity

FLOPS = 805306368

F32 = mybir.dt.float32
BF16 = mybir.dt.bfloat16
I32 = mybir.dt.int32
U32 = mybir.dt.uint32
U16 = mybir.dt.uint16
U8 = mybir.dt.uint8
FP8X4 = mybir.dt.float8_e4m3fn_x4
FP4X4 = mybir.dt.float4_e2m1fn_x4
ALU = mybir.AluOpType
COPY = mybir.ActivationFunctionType.Copy
RELU = mybir.ActivationFunctionType.Relu

P = 128
PACK = 4
LAST = PACK - 1
S = 512
HALF = S // 2
PAGE = 1024
T = 1024
G = 2048
QUADRANT = 32
ROWS_PER_QUADRANT = 4
TABLE_ROW_STEP = 8
LIST_GROUP = 16
LINE = 16
PSUM_BANKS = 8
NQ = 4
QW = S // NQ
H2_FACTOR = 0.0625


def tile_picked_dhzmhswapdpagsn_none_p_kernel(
    tc, x_words, x_scales, w1_words, w1_scales, gs, d_words, d_scales, offs, n1, n2, n3, k1, k2, hz, n4, n5, n6, out
):
    nc = tc.nc
    with ExitStack() as ctx:
        held = ctx.enter_context(tc.tile_pool(name="lists", bufs=1))
        pool = ctx.enter_context(tc.tile_pool(name="work", bufs=1))
        psum = ctx.enter_context(tc.psum_pool(name="psum", bufs=PSUM_BANKS))

        def sb(name, width, dtype, after=None):
            return pool.tile([P, width], dtype, name=name, tag=after or name, align_bytes=64)

        def new_bank():
            return psum.tile([P, S], F32, name="bank", tag="bank")

        def load_list(name, src):
            tile = held.tile(list(src.shape), U16, name=name)
            nc.sync.dma_start(tile[:], src)
            return tile

        def entries(lst, first, count):
            return lst[:, first // LIST_GROUP : (first + count) // LIST_GROUP]

        def zeroed_bytes(engine, name, width):
            tile = sb(name, width, U8)
            engine.memset(tile[:].bitcast(I32), 0)
            return tile

        def place_rows(plane, picked):
            for i in range(ROWS_PER_QUADRANT):
                nc.sync.dma_start(
                    plane[:].bitcast(I32)[i:P:QUADRANT, :],
                    picked[:].bitcast(I32)[TABLE_ROW_STEP * i : P : QUADRANT, :],
                )

        def deal(engine_copy, dst, src, element_bytes):
            run = LINE // element_bytes
            engine_copy(
                dst.rearrange("p (t c i) -> p c t i", t=PACK, i=run),
                src.rearrange("p (c i t) -> p c t i", t=PACK, i=run),
            )

        x_byte_table = zeroed_bytes(nc.gpsimd, "x_byte_table", T)
        w1_raw_plane = zeroed_bytes(nc.gpsimd, "w1_raw_plane", S)
        d_byte_table = zeroed_bytes(nc.vector, "d_byte_table", G)
        xq_plane = zeroed_bytes(nc.vector, "xq_plane", S)
        xh_plane = zeroed_bytes(nc.vector, "xh_plane", S)
        dk_planes = zeroed_bytes(nc.vector, "dk_planes", 2 * S)
        minus_one = sb("minus_one", HALF, F32)
        nc.vector.memset(minus_one[:], -1.0)
        identity = sb("identity", P, F32)
        make_identity(nc, identity[:])

        offs_l = load_list("offs_l", offs)
        nc.sync.dma_start(x_byte_table[:].bitcast(I32)[0:P:TABLE_ROW_STEP, :], x_scales[0].bitcast(I32))
        x_word_table = sb("x_word_table", T, U32)
        nc.sync.dma_start(x_word_table[:].bitcast(I32), x_words[0].rearrange("p n t -> p (n t)").bitcast(I32))
        w1_raw = sb("w1_raw", 2 * S, U8)
        nc.sync.dma_start(w1_raw[:].bitcast(I32), w1_words[0].bitcast(I32))
        for quad in range(P // QUADRANT):
            nc.sync.dma_start(
                w1_raw_plane[:].bitcast(I32)[QUADRANT * quad : QUADRANT * quad + ROWS_PER_QUADRANT, :],
                w1_scales[0, ROWS_PER_QUADRANT * quad : ROWS_PER_QUADRANT * (quad + 1), :].bitcast(I32),
            )
        hz_l = load_list("hz_l", hz)
        nc.sync.dma_start(d_byte_table[:].bitcast(I32)[0:P:TABLE_ROW_STEP, :], d_scales[0].bitcast(I32))
        k1_l = load_list("k1_l", k1)
        k2_l = load_list("k2_l", k2)

        xq_bytes = sb("xq_bytes", S, U8)
        nc.vector.tensor_copy(xq_bytes[:], x_byte_table[:].indirect(offs_l[:]))
        place_rows(xq_plane, xq_bytes)
        xq_words = sb("xq_words", S, U32)
        nc.vector.tensor_copy(xq_words[:], x_word_table[:].indirect(offs_l[:]))
        w1_dealt = sb("w1_dealt", 2 * S, U8)
        deal(nc.scalar.copy, w1_dealt[:].bitcast(U16), w1_raw[:].bitcast(U16), 2)
        w1_plane = sb("w1_plane", S, U8)
        deal(nc.gpsimd.tensor_copy, w1_plane[:], w1_raw_plane[:], 1)

        n2_l = load_list("n2_l", n2)
        n1_l = load_list("n1_l", n1)
        n3_l = load_list("n3_l", n3)
        gs_sb = sb("gs_sb", PACK, F32)
        nc.sync.dma_start(gs_sb[:], gs.rearrange("(p t) o -> p (t o)", t=PACK))
        d_word_table = sb("d_word_table", G, U32)
        nc.sync.dma_start(d_word_table[:].bitcast(I32), d_words[0].rearrange("p n t -> p (n t)").bitcast(I32))

        xh_bytes = sb("xh_bytes", S, U8)
        nc.vector.tensor_copy(xh_bytes[:], x_byte_table[:].indirect(hz_l[:]))
        place_rows(xh_plane, xh_bytes)
        dk_bytes = sb("dk_bytes", 2 * S, U8)
        dk_bytes_dealt = sb("dk_bytes_dealt", 2 * S, U8)
        for a, lst in enumerate((k1_l, k2_l)):
            nc.vector.tensor_copy(dk_bytes[:, a * S : (a + 1) * S], d_byte_table[:].indirect(lst[:]))
        for a in range(2):
            deal(nc.vector.tensor_copy, dk_bytes_dealt[:, a * S : (a + 1) * S], dk_bytes[:, a * S : (a + 1) * S], 1)
        place_rows(dk_planes, dk_bytes_dealt)

        n6_l = load_list("n6_l", n6)
        n4_l = load_list("n4_l", n4)
        n5_l = load_list("n5_l", n5)

        y_banks = []
        for t in range(PACK):
            bank = new_bank()
            nc.tensor.matmul_mx(
                bank[:],
                lhsT=w1_dealt[:, 2 * P * t : 2 * P * (t + 1)].bitcast(FP4X4),
                lhsT_scale=w1_plane[:, P * t : P * (t + 1)],
                rhs=xq_words[:].bitcast(FP8X4),
                rhs_scale=xq_plane[:],
                start=True,
                stop=True,
            )
            y_banks.append(bank)

        y, pa, minus_pb, ub, larger = {}, {}, {}, {}, {}
        z_bf = [sb("z_bf%d" % q, QW * PACK, BF16) for q in range(NQ)]
        z_words = sb("z_words", S, U32)
        z_plane = sb("z_plane", S, U8)

        def drain_y(t):
            y[t] = sb("y%d" % t, S, F32)
            nc.scalar.copy(y[t][:], y_banks[t][:])

        def put_pb(t):
            minus_pb[t] = sb("pb%d" % t, HALF, F32)
            nc.scalar.activation(minus_pb[t][:], y[t][:].indirect(n2_l[:]), COPY, scale=-1.0)
            ub[t] = sb("ub%d" % t, S, F32)
            nc.vector.tensor_tensor(ub[t][:].indirect(n1_l[:]), minus_pb[t][:], minus_one[:], ALU.mult)

        def put_rb(t):
            pa[t] = sb("pa%d" % t, HALF, F32)
            nc.scalar.activation(pa[t][:], y[t][:].indirect(n1_l[:]), COPY)
            nc.vector.tensor_tensor(ub[t][:].indirect(n2_l[:]), pa[t][:], minus_pb[t][:], ALU.add)

        def take_larger(t):
            fetched = sb("fetched%d" % t, S, F32)
            for h in range(2):
                nc.scalar.activation(
                    fetched[:, h * HALF : (h + 1) * HALF], ub[t][:].indirect(entries(n3_l, h * HALF, HALF)), COPY
                )
            larger[t] = sb("larger%d" % t, S, F32)
            nc.vector.scalar_tensor_tensor(larger[t][:], fetched[:], 0.5, ub[t][:], ALU.mult, ALU.max)

        pairs = sb("pairs", PACK * S, BF16)
        pair_halves = pairs[:].rearrange("p (q u j e) -> p u e q j", q=NQ, u=2, e=2)
        whole_pairs = pairs[:].bitcast(F32).rearrange("p (q u j) -> p q j u", q=NQ, u=2)

        def weigh(t):
            nc.scalar.activation(
                pair_halves[:, t // 2, t % 2, :, :],
                larger[t][:].rearrange("p (q j) -> p q j", q=NQ),
                COPY,
                scale=gs_sb[:, t : t + 1],
            )

        def pick_d_words(name, lst, after):
            picked = sb(name, S, U32, after)
            nc.vector.tensor_copy(picked[:], d_word_table[:].indirect(lst[:]))
            return picked

        def deal_d_words(name, picked, after):
            dealt = sb(name, S, U32, after)
            deal(nc.vector.tensor_copy, dealt[:].bitcast(I32), picked[:].bitcast(I32), 4)
            return dealt

        def pick_xh_words(q, after):
            picked = sb("xh_words%d" % q, QW, U32, after)
            nc.vector.tensor_copy(picked[:], x_word_table[:].indirect(entries(hz_l, q * QW, QW)))
            return picked

        drain_y(0)
        put_pb(0)
        drain_y(1)
        put_pb(1)
        put_rb(0)
        put_rb(1)
        drain_y(2)
        put_pb(2)
        drain_y(3)
        take_larger(0)
        put_rb(2)
        dk1_picked = pick_d_words("dk1_picked", k1_l, after="y2")
        take_larger(1)
        put_pb(3)
        weigh(0)
        dk1_words = deal_d_words("dk1_words", dk1_picked, after="larger0")
        take_larger(2)
        put_rb(3)
        dk2_picked = pick_d_words("dk2_picked", k2_l, after="y3")
        weigh(1)
        weigh(2)

        h2 = [sb("h2_%d" % t, S, F32) for t in range(PACK)]
        ds = [sb("ds%d" % t, PAGE, F32) for t in range(PACK)]

        def hashed_pass(dst, t, q, start):
            rows = slice(P * t, P * (t + 1))
            cols = slice(QW * q, QW * (q + 1))
            nc.tensor.matmul_mx(
                dst,
                lhsT=dk2_words[:, rows].bitcast(FP8X4),
                lhsT_scale=dk_planes[:, S + P * t : S + P * (t + 1)],
                rhs=xh_words[q][:].bitcast(FP8X4),
                rhs_scale=xh_plane[:, cols],
                start=start,
                stop=False,
            )

        def z_pass(dst, t, cols):
            rows = slice(P * t, P * (t + 1))
            nc.tensor.matmul_mx(
                dst,
                lhsT=dk1_words[:, rows].bitcast(FP8X4),
                lhsT_scale=dk_planes[:, rows],
                rhs=z_words[:, cols].bitcast(FP8X4),
                rhs_scale=z_plane[:, cols],
                start=False,
                stop=True,
            )

        last_larger = {}

        def take_last_larger(q):
            cols = slice(QW * q, QW * (q + 1))
            fetched = sb("last_fetched%d" % q, QW, F32)
            nc.scalar.activation(fetched[:], ub[LAST][:].indirect(entries(n3_l, q * QW, QW)), COPY)
            last_larger[q] = sb("last_larger%d" % q, QW, F32)
            nc.vector.scalar_tensor_tensor(last_larger[q][:], fetched[:], 0.5, ub[LAST][:, cols], ALU.mult, ALU.max)

        def weigh_last_and_weave(q):
            nc.scalar.activation(
                pair_halves[:, LAST // 2, LAST % 2, q, :], last_larger[q][:], COPY, scale=gs_sb[:, LAST : LAST + 1]
            )
            nc.vector.tensor_copy(z_bf[q][:].bitcast(F32).rearrange("p (j u) -> p j u", u=2), whole_pairs[:, q, :, :])

        def quantise(q):
            cols = slice(QW * q, QW * (q + 1))
            nc.vector.quantize_mx(z_words[:, cols].bitcast(FP8X4), z_plane[:, cols], z_bf[q][:])

        def send_first_tile(q):
            cols = slice(QW * q, QW * (q + 1))
            bank = new_bank()
            hashed_pass(bank[:, 0:QW], 0, q, True)
            z_pass(bank[:, 0:QW], 0, cols)
            nc.scalar.mul(h2[0][:, cols], bank[:, 0:QW], H2_FACTOR)
            nc.vector.tensor_copy(ds[0][:].indirect(entries(n6_l, q * QW, QW)), h2[0][:, cols])

        for q in range(NQ):
            take_last_larger(q)
        weigh_last_and_weave(0)
        for q in range(NQ):
            if q + 1 < NQ:
                weigh_last_and_weave(q + 1)
            quantise(q)
        dk2_words = deal_d_words("dk2_words", dk2_picked, after="last_fetched0")
        xh_words = [
            pick_xh_words(q, after)
            for q, after in enumerate(("last_fetched1", "last_fetched2", "last_fetched3", "last_larger0"))
        ]
        for q in range(NQ):
            send_first_tile(q)

        for t in range(1, PACK):
            bank = new_bank()
            for q in range(NQ):
                hashed_pass(bank[:, QW * q : QW * (q + 1)], t, q, q == 0)
            z_pass(bank[:], t, slice(0, S))
            nc.scalar.mul(h2[t][:], bank[:], H2_FACTOR)

        excess, page = {}, {}
        out_rows = out.rearrange("(p t) w -> t p w", t=PACK)

        def send(t):
            nc.vector.tensor_copy(ds[t][:].indirect(n6_l[:]), h2[t][:])

        def put_ds(t):
            page[t] = sb("page%d" % t, PAGE, F32, after="larger0" if t == 0 else None)
            nc.vector.tensor_copy(page[t][:].indirect(n4_l[:]), ds[t][:, 0:S])

        def find_excess(t):
            minus_h2 = sb("minus_h2_%d" % t, S, F32)
            nc.scalar.mul(minus_h2[:], h2[t][:], -1.0)
            turned = new_bank()
            for c in range(S // P):
                cols = slice(P * c, P * (c + 1))
                for term, first in ((minus_h2, True), (ds[t], False)):
                    nc.tensor.matmul(
                        turned[:, cols], term[:, cols], identity[:], start=first, stop=not first, is_transpose=True
                    )
            clipped = sb("clipped%d" % t, S, F32)
            nc.scalar.activation(clipped[:], turned[:], RELU)
            back = new_bank()
            for c in range(S // P):
                cols = slice(P * c, P * (c + 1))
                nc.tensor.transpose(back[:, cols], clipped[:, cols], identity[:])
            excess[t] = sb("excess%d" % t, S, F32)
            nc.scalar.copy(excess[t][:], back[:])

        def put_up(t):
            nc.vector.tensor_tensor(page[t][:].indirect(n5_l[:]), h2[t][:], excess[t][:], ALU.add)
            nc.sync.dma_start(out_rows[t], page[t][:])

        find_excess(0)
        send(1)
        find_excess(1)
        put_ds(0)
        send(2)
        find_excess(2)
        put_up(0)
        put_ds(1)
        send(3)
        find_excess(3)
        put_up(1)
        put_ds(2)
        put_ds(3)
        put_up(2)
        put_up(3)
